import numpy as np
import ml_dtypes


def mxq(x, axis, fmt="e4m3"):
    dtype, down = {"e4m3": (ml_dtypes.float8_e4m3fn, 7), "e5m2": (ml_dtypes.float8_e5m2, 14)}[fmt]
    v = np.moveaxis(np.asarray(x, np.float32).astype(ml_dtypes.bfloat16).astype(np.float64), axis, -1)
    blocks = v.reshape(v.shape[:-1] + (-1, 32))
    amax = np.abs(blocks).max(-1, keepdims=True)
    byte = np.maximum(np.where(amax > 0, np.frexp(amax)[1] - 1 + 127, 0) - down, 1)
    scale = np.exp2(byte - 127.0)
    codes = (blocks / scale).astype(np.float32).astype(dtype).astype(np.float64)
    return np.moveaxis((codes * scale).reshape(v.shape), -1, axis)


WIDE = False


def mx_kscale(k):
    if not WIDE:
        return np.ones(k)
    levels = np.array([10, -10, 5, -5, 0])
    if k % 512:
        return np.exp2(np.random.permutation(np.resize(levels, k // 32))).repeat(32)
    a = np.empty((k // 512, 16))
    for p in range(k // 512):
        a[p, :8] = np.random.permutation(np.resize(levels, 8))
        for g in range(8):
            far = levels[np.abs(levels - a[p, g]) >= 10]
            a[p, g + 8] = far[np.random.randint(len(far))]
    return np.exp2(a.ravel()).repeat(32)


def f64(x):
    return np.asarray(x).astype(np.float64)


def striped(idx):
    return np.tile(idx.reshape(-1, 16).T, (8, 1)).astype(np.uint16)


def unstriped(offs):
    return offs[:16].T.reshape(-1).astype(np.int64)


E2M1 = np.array([0.0, 0.5, 1.0, 1.5, 2.0, 3.0, 4.0, 6.0, -0.0, -0.5, -1.0, -1.5, -2.0, -3.0, -4.0, -6.0])


def pack_weight(w, fmt):
    k, n = w.shape
    w = f64(np.asarray(w, np.float32).astype(ml_dtypes.bfloat16)).reshape(k // 32, 32, n)
    amax = np.abs(w).max(1)
    if fmt == "e4m3":
        byte = np.frexp(amax)[1] - 1 + 127 - 7
    else:
        mant, ex = np.frexp(amax / 6.0)
        byte = np.where(mant > 0.5, ex, ex - 1) + 127
    byte = np.clip(np.where(amax > 0, byte, 1), 1, 254)
    scaled = (w * np.exp2(127.0 - byte)[:, None, :]).reshape(k, n).astype(np.float32)
    by_word = np.ascontiguousarray(scaled.reshape(k // 512, 128, 4, n).transpose(0, 1, 3, 2))
    if fmt == "e4m3":
        words = by_word.astype(ml_dtypes.float8_e4m3fn).view(np.uint8)
    else:
        c = by_word.astype(ml_dtypes.float4_e2m1fn).view(np.uint8) & 0xF
        words = (c[..., 0::2] | (c[..., 1::2] << 4)).reshape(k // 512, 128, 2 * n)
    return np.ascontiguousarray(words), np.ascontiguousarray(byte.astype(np.uint8).reshape(k // 512, 16, n))


def unpack_weight(words, scales, fmt):
    g, _, n = scales.shape
    words = np.ascontiguousarray(words).reshape(g, 128, n, -1)
    if fmt == "e4m3":
        vals = words.view(ml_dtypes.float8_e4m3fn).astype(np.float64)
    else:
        nib = np.empty((g, 128, n, 4), np.uint8)
        nib[..., 0::2] = words & 0xF
        nib[..., 1::2] = words >> 4
        vals = E2M1[nib]
    vals = vals * np.repeat(np.exp2(scales.astype(np.float64) - 127.0), 8, axis=1)[..., None]
    return vals.transpose(0, 1, 3, 2).reshape(g * 512, n)


def gelu(v):
    return 0.5 * v * (1.0 + np.tanh(np.sqrt(2.0 / np.pi) * (v + 0.044715 * v**3)))


K, M, H, N, T, T2, T3, S = 1024, 512, 1024, 512, 2048, 1024, 1024, 512

def setup_inputs():
    n = np.random.standard_normal
    s = mx_kscale(K)[:, None]
    s2 = mx_kscale(M)[:, None]
    u = mx_kscale(H)[:, None]
    tab_words, tab_scales = pack_weight(n((K, T)) * s, "e4m3")
    tab2_words, tab2_scales = pack_weight(n((M, T2)) * s2, "e4m3")
    tab3_words, tab3_scales = pack_weight(n((M, T3)) * s2, "e2m1")
    w2_words, w2_scales = pack_weight(n((M, H)) / np.sqrt(M) / s2, "e2m1")
    w4_words, w4_scales = pack_weight(2.0 * n((H, N)) / np.sqrt(H) / u, "e4m3")
    return {
        "tab_words": tab_words, "tab_scales": tab_scales,
        "tab2_words": tab2_words, "tab2_scales": tab2_scales,
        "tab3_words": tab3_words, "tab3_scales": tab3_scales,
        "offs": striped(np.random.permutation(T)[:S]),
        "offs2": striped(np.random.permutation(T2)[:S]),
        "offs3": striped(np.random.permutation(T3)[:S]),
        "w1": (n((K, H)) / np.sqrt(K) / s * u.T).astype(np.float32),
        "w2_words": w2_words, "w2_scales": w2_scales,
        "w3": (n((M, H)) / np.sqrt(M) / s2).astype(np.float32),
        "w4_words": w4_words, "w4_scales": w4_scales,
    }

def reference(tab_words, tab_scales, tab2_words, tab2_scales, tab3_words, tab3_scales,
              offs, offs2, offs3, w1, w2_words, w2_scales, w3, w4_words, w4_scales):
    v = unpack_weight(tab_words, tab_scales, "e4m3")[:, unstriped(offs)]
    v2 = unpack_weight(tab2_words, tab2_scales, "e4m3")[:, unstriped(offs2)]
    v3 = unpack_weight(tab3_words, tab3_scales, "e2m1")[:, unstriped(offs3)]
    a = mxq(f64(w1), 0, "e4m3").T @ v
    b = unpack_weight(w2_words, w2_scales, "e2m1").T @ v2
    d = mxq(f64(w3), 0, "e4m3").T @ v3
    h = a / (1.0 + b * b + np.abs(d))
    w4 = unpack_weight(w4_words, w4_scales, "e4m3")
    return w4.T @ mxq(h, 0, "e4m3")

@@ -1,0 +1,257 @@
+from contextlib import ExitStack
+
+import concourse.mybir as mybir
+from concourse.masks import make_identity
+
+K, M, H, N, T, T2, T3, S = 1024, 512, 1024, 512, 2048, 1024, 1024, 512
+FLOPS = 2 * S * H * (K + 2 * M + N)
+
+F32 = mybir.dt.float32
+BF16 = mybir.dt.bfloat16
+I32 = mybir.dt.int32
+U32 = mybir.dt.uint32
+U16 = mybir.dt.uint16
+U8 = mybir.dt.uint8
+FP8X4 = mybir.dt.float8_e4m3fn_x4
+FP4X4 = mybir.dt.float4_e2m1fn_x4
+ACT = mybir.ActivationFunctionType
+ALU = mybir.AluOpType
+
+P = 128
+PACK = 4
+KP = P * PACK
+KPASS = K // KP
+HPASS = H // KP
+JT = S // P
+JH = S // 2
+
+
+def tile_list_cosolvent_well_quotient_kernel(
+    tc, tab_words, tab_scales, tab2_words, tab2_scales, tab3_words, tab3_scales,
+    offs, offs2, offs3, w1, w2_words, w2_scales, w3, w4_words, w4_scales, out,
+):
+    nc = tc.nc
+    with ExitStack() as ctx:
+        lists = ctx.enter_context(tc.tile_pool(name="lists", bufs=1))
+        keep = ctx.enter_context(tc.tile_pool(name="keep", bufs=1))
+        ring = ctx.enter_context(tc.tile_pool(name="ring", bufs=3))
+        psum = ctx.enter_context(tc.psum_pool(name="psum", bufs=2))
+
+        def held(name, cols, dtype, slot=""):
+            return keep.tile([P, cols], dtype, name=name, tag=slot, align_bytes=64)
+
+        def zeroed_plane(engine, name, cols, slot=""):
+            plane = held(name, cols, U8, slot)
+            engine.memset(plane[:].bitcast(I32), 0)
+            return plane
+
+        def load_scales(queue, plane, scales):
+            passes = scales.shape[0]
+            for q in range(4):
+                queue.dma_start(
+                    out=plane[32 * q : 32 * q + 4 * passes, :].bitcast(I32),
+                    in_=scales[:, 4 * q : 4 * q + 4, :].bitcast(I32),
+                )
+
+        def load_words(name, cols, dtype, src, slot=""):
+            words = held(name, cols, dtype, slot)
+            nc.sync.dma_start(out=words[:].bitcast(I32), in_=src.bitcast(I32))
+            return words
+
+        def load_list(name, src):
+            tile = lists.tile([P, S // 16], U16, name=name)
+            nc.sync.dma_start(tile[:], src)
+            return tile
+
+        def load_weight(name, w, a, g):
+            raw = keep.tile([P, PACK, KP], F32, name=name)
+            src = w[a * KP : (a + 1) * KP, g * KP : (g + 1) * KP]
+            nc.sync.dma_start(out=raw[:], in_=src.rearrange("(p i) c -> p i c", i=PACK))
+            return raw
+
+        def gather(name, window, offsets, dtype, slot=""):
+            picked = held(name, S, dtype, slot)
+            nc.vector.tensor_copy(picked[:], window[:].indirect(offsets[:]))
+            return picked
+
+        def quantize(name, grouped):
+            cols = grouped.shape[1] // PACK
+            codes = held(name + "_codes", cols, U32)
+            plane = held(name + "_plane", cols, U8)
+            nc.vector.quantize_mx(out=codes[:].bitcast(FP8X4), scales=plane[:], in_=grouped[:])
+            return codes, plane
+
+        tab2_s = zeroed_plane(nc.vector, "tab2_s", T2)
+        w2_s = zeroed_plane(nc.gpsimd, "w2_s", H)
+        tab3_s = zeroed_plane(nc.vector, "tab3_s", T3, "Z")
+        tab_s = zeroed_plane(nc.gpsimd, "tab_s", T)
+        w4_s = zeroed_plane(nc.vector, "w4_s", N)
+
+        warm = keep.tile([P, 2], F32, name="warm")
+        nc.vector.memset(warm[:, 0:1], 1.0)
+        nc.scalar.activation(out=warm[:, 1:2], in_=warm[:, 0:1], func=ACT.Abs_reciprocal_sqrt)
+
+        ident = keep.tile([P, P], F32, name="ident")
+        make_identity(nc, ident[:])
+        list2 = load_list("list2", offs2)
+        tab2_w = load_words("tab2_w", T2, U32, tab2_words[0].rearrange("p t i -> p (t i)"))
+        load_scales(nc.sync, tab2_s, tab2_scales)
+        w2_w = load_words("w2_w", H, U16, w2_words[0])
+        w3_raw = [load_weight("w3_raw0", w3, 0, 0)]
+        load_scales(nc.sync, w2_s, w2_scales)
+        tab3_w = load_words("tab3_w", T3, U16, tab3_words[0])
+        list3 = load_list("list3", offs3)
+        w3_raw.append(load_weight("w3_raw1", w3, 0, 1))
+        load_scales(nc.sync, tab3_s, tab3_scales)
+        w1_raw = {(a, 0): load_weight("w1_raw%d0" % a, w1, a, 0) for a in range(KPASS)}
+        list1 = load_list("list1", offs)
+        load_scales(nc.sync, tab_s, tab_scales)
+        tab_w = [
+            load_words("tab_w%d" % a, T, U32, tab_words[a].rearrange("p t i -> p (t i)"), "D" if a == 0 else "")
+            for a in range(KPASS)
+        ]
+        for a in range(KPASS):
+            w1_raw[a, 1] = load_weight("w1_raw%d1" % a, w1, a, 1)
+        w4_w = keep.tile([P, HPASS, N], U32, name="w4_w", align_bytes=64)
+        nc.sync.dma_start(out=w4_w[:].bitcast(I32), in_=w4_words.rearrange("g p n i -> p g (n i)").bitcast(I32))
+        load_scales(nc.sync, w4_s, w4_scales)
+
+        def round_w3(copy, g):
+            grouped = held("w3_bf%d" % g, PACK * KP, BF16, "XZ"[g])
+            copy(
+                out=grouped[:].rearrange("p (c e i) -> p c i e", e=4, i=PACK),
+                in_=w3_raw[g][:].rearrange("p i (c e) -> p c i e", e=4),
+            )
+            return grouped
+
+        def round_w1(copy, a, g):
+            grouped = held("w1_bf%d%d" % (a, g), PACK * KP, BF16, "G%d" % a if g == 1 else "ZY"[a])
+            copy(
+                out=grouped[:].rearrange("p (t m i) -> p m i t", t=PACK, i=PACK),
+                in_=w1_raw[a, g][:].rearrange("p i (m t) -> p m i t", t=PACK),
+            )
+            return grouped
+
+        def square_b(g, jt):
+            j = slice(jt * P, (jt + 1) * P)
+            r = slice(g * KP, (g + 1) * KP)
+            b_ps = psum.tile([P, KP], F32, tag="wide", bufs=4, name="b_ps")
+            nc.tensor.matmul_mx(
+                out=b_ps[:], lhsT=v2[:, j].bitcast(FP8X4), lhsT_scale=v2_s[:, j],
+                rhs=w2_w[:, r].bitcast(FP4X4), rhs_scale=w2_s[:, r], start=True, stop=True,
+            )
+            b2[g, jt] = keep.tile([P, PACK, P], F32, name="b2_%d%d" % (g, jt))
+            nc.scalar.activation(out=b2[g, jt][:], in_=b_ps[:].rearrange("p (m t) -> p t m", t=PACK), func=ACT.Square)
+
+        def abs_d(g, jt):
+            j = slice(jt * P, (jt + 1) * P)
+            d_ps = psum.tile([P, KP], F32, tag="wide", bufs=4, name="d_ps")
+            codes, plane = w3_q[g]
+            nc.tensor.matmul_mx(
+                out=d_ps[:], lhsT=v3[:, j].bitcast(FP4X4), lhsT_scale=v3_s[:, j],
+                rhs=codes[:].bitcast(FP8X4), rhs_scale=plane[:], start=True, stop=True,
+            )
+            dabs[g, jt] = keep.tile([P, PACK, P], F32, name="dabs_%d%d" % (g, jt), tag="dabs", bufs=2)
+            nc.scalar.activation(out=dabs[g, jt][:], in_=d_ps[:].rearrange("p (m t) -> p t m", t=PACK), func=ACT.Abs)
+
+        def invert(g, jt, bank):
+            x_ps = quad[bank]
+            for t in range(PACK):
+                nc.tensor.matmul(x_ps[:, t, :], b2[g, jt][:, t, :], ident[:], start=True, stop=False, is_transpose=True)
+                nc.tensor.matmul(x_ps[:, t, :], dabs[g, jt][:, t, :], ident[:], start=False, stop=True, is_transpose=True)
+            root = ring.tile([P, P, PACK], F32, name="root")
+            nc.scalar.activation(
+                out=root[:], in_=x_ps[:].rearrange("p t j -> p j t"), func=ACT.Abs_reciprocal_sqrt, bias=1.0,
+            )
+            rec[g, jt] = keep.tile([P, P, PACK], F32, name="rec%d%d" % (g, jt))
+            nc.scalar.activation(out=rec[g, jt][:], in_=root[:], func=ACT.Square)
+
+        def prepare_w1(a, g):
+            w1_q[a, g] = quantize("w1_q%d%d" % (a, g), round_w1(nc.vector.tensor_copy, a, g))
+
+        def quotient(g, jt, bank):
+            jh, u = divmod(jt, JH // P)
+            if u == 0:
+                h_bf[g, jh] = held("h_bf%d%d" % (g, jh), JH * PACK, BF16, "G%d" % jh if g == 0 else "")
+            j = slice(jt * P, (jt + 1) * P)
+            a_ps = quad[bank]
+            for t in range(PACK):
+                cols = slice(t * P, (t + 1) * P)
+                for a in range(KPASS):
+                    codes, plane = w1_q[a, g]
+                    nc.tensor.matmul_mx(
+                        out=a_ps[:, t, :], lhsT=codes[:, cols].bitcast(FP8X4), lhsT_scale=plane[:, cols],
+                        rhs=v1[a][:, j].bitcast(FP8X4), rhs_scale=v1_s[4 * a :, j],
+                        start=(a == 0), stop=(a == KPASS - 1),
+                    )
+            nc.vector.tensor_tensor(
+                out=h_bf[g, jh][:, u * KP : (u + 1) * KP].rearrange("p (j t) -> p j t", t=PACK),
+                in0=a_ps[:].rearrange("p t j -> p j t"), in1=rec[g, jt][:], op=ALU.mult,
+            )
+
+        def quantize_h(g, jh):
+            h_q[g, jh] = quantize("h_q%d%d" % (g, jh), h_bf[g, jh])
+
+        def features(g, jh):
+            codes, plane = h_q[g, jh]
+            for nt in range(N // P):
+                n = slice(nt * P, (nt + 1) * P)
+                nc.tensor.matmul_mx(
+                    out=o_ps[jh, nt // 2][:, nt % 2, :], lhsT=w4_w[:, g, n].bitcast(FP8X4), lhsT_scale=w4_s[4 * g :, n],
+                    rhs=codes[:].bitcast(FP8X4), rhs_scale=plane[:],
+                    start=(g == 0 and nt % 2 == 0), stop=(g == HPASS - 1 and nt % 2 == 1),
+                )
+
+        def store(jh):
+            for pair, copy in enumerate((nc.scalar.copy, nc.vector.tensor_copy if jh == 1 else nc.scalar.copy)):
+                res = keep.tile([P, 2, JH], F32, name="res%d%d" % (jh, pair))
+                copy(out=res[:], in_=o_ps[jh, pair][:])
+                dst = out[pair * 2 * P : (pair + 1) * 2 * P, jh * JH : (jh + 1) * JH]
+                nc.sync.dma_start(out=dst.rearrange("(k p) j -> p k j", p=P), in_=res[:])
+
+        b2, dabs, rec, w1_q, h_bf, h_q = {}, {}, {}, {}, {}, {}
+        quad = [psum.tile([P, PACK, P], F32, bufs=1, name="quad%d" % k) for k in range(4)]
+        v2 = gather("v2", tab2_w, list2, U32)
+        v2_s = gather("v2_s", tab2_s, list2, U8)
+        w3_q = [quantize("w3_q0", round_w3(nc.vector.tensor_copy, 0))]
+        v3 = gather("v3", tab3_w, list3, U16)
+        v3_s = gather("v3_s", tab3_s, list3, U8, "X")
+        for g in range(HPASS):
+            for jt in range(JT):
+                square_b(g, jt)
+        w3_q.append(quantize("w3_q1", round_w3(nc.vector.tensor_copy, 1)))
+        abs_d(0, 0)
+        abs_d(0, 1)
+        for jt in range(JT):
+            invert(0, jt, jt)
+            abs_d(*divmod(jt + 2, JT))
+        prepare_w1(0, 0)
+        prepare_w1(1, 0)
+        v1_s = gather("v1_s", tab_s, list1, U8, "Z")
+        v1 = [gather("v1_%d" % a, tab_w[a], list1, U32, "YD"[a]) for a in range(KPASS)]
+        quotient(0, 0, 1)
+        quotient(0, 1, 2)
+        quantize_h(0, 0)
+        invert(1, 0, 0)
+        abs_d(1, 2)
+        quotient(0, 2, 3)
+        prepare_w1(0, 1)
+        invert(1, 1, 1)
+        abs_d(1, 3)
+        quotient(0, 3, 0)
+        quantize_h(0, 1)
+        invert(1, 2, 2)
+        invert(1, 3, 3)
+        prepare_w1(1, 1)
+        o_ps = {}
+        for jh in range(2):
+            for pair in range(2):
+                o_ps[jh, pair] = psum.tile([P, 2, JH], F32, tag="wide", bufs=4, name="o_ps%d%d" % (jh, pair))
+        for jh in range(2):
+            features(0, jh)
+        for jh in range(2):
+            quotient(1, 2 * jh, 2 * jh)
+            quotient(1, 2 * jh + 1, 2 * jh + 1)
+            quantize_h(1, jh)
+            features(1, jh)
+            store(jh)

@@ -124,69 +124,71 @@ def tile_list_cosolvent_well_quotient_kernel(
             )
             return grouped
 
-        def round_w1(copy, a, g):
-            grouped = held("w1_bf%d%d" % (a, g), PACK * KP, BF16, "G%d" % a if g == 1 else "ZY"[a])
-            copy(
-                out=grouped[:].rearrange("p (t m i) -> p m i t", t=PACK, i=PACK),
-                in_=w1_raw[a, g][:].rearrange("p i (m t) -> p m i t", t=PACK),
-            )
+        def round_w1(a, g):
+            grouped = held("w1_bf%d%d" % (a, g), PACK * KP, BF16, "rec0%d" % (2 * a) if g == 1 else "ZY"[a])
+            dst = grouped[:].rearrange("p (t m i) -> p m i t", t=PACK, i=PACK)
+            src = w1_raw[a, g][:].rearrange("p i (m t) -> p m i t", t=PACK)
+            if (a, g) == (KPASS - 1, HPASS - 1):
+                nc.vector.tensor_copy(out=dst[:, :, :, 0:2], in_=src[:, :, :, 0:2])
+                nc.scalar.copy(out=dst[:, :, :, 2:4], in_=src[:, :, :, 2:4])
+            else:
+                nc.vector.tensor_copy(out=dst, in_=src)
             return grouped
 
-        def square_b(g, jt):
+        def square_b(g, jt, b_ps):
             j = slice(jt * P, (jt + 1) * P)
             r = slice(g * KP, (g + 1) * KP)
-            b_ps = psum.tile([P, KP], F32, tag="wide", bufs=4, name="b_ps")
             nc.tensor.matmul_mx(
                 out=b_ps[:], lhsT=v2[:, j].bitcast(FP8X4), lhsT_scale=v2_s[:, j],
                 rhs=w2_w[:, r].bitcast(FP4X4), rhs_scale=w2_s[:, r], start=True, stop=True,
             )
-            b2[g, jt] = keep.tile([P, PACK, P], F32, name="b2_%d%d" % (g, jt))
+            b2[g, jt] = keep.tile([P, PACK, P], F32, name="b2_%d%d" % (g, jt), tag="b2_%d%d" % (g, jt), align_bytes=64)
             nc.scalar.activation(out=b2[g, jt][:], in_=b_ps[:].rearrange("p (m t) -> p t m", t=PACK), func=ACT.Square)
 
         def abs_d(g, jt):
+            d_ps = bank[jt]
             j = slice(jt * P, (jt + 1) * P)
-            d_ps = psum.tile([P, KP], F32, tag="wide", bufs=4, name="d_ps")
             codes, plane = w3_q[g]
             nc.tensor.matmul_mx(
                 out=d_ps[:], lhsT=v3[:, j].bitcast(FP4X4), lhsT_scale=v3_s[:, j],
                 rhs=codes[:].bitcast(FP8X4), rhs_scale=plane[:], start=True, stop=True,
             )
-            dabs[g, jt] = keep.tile([P, PACK, P], F32, name="dabs_%d%d" % (g, jt), tag="dabs", bufs=2)
+            dabs[g, jt] = keep.tile([P, PACK, P], F32, name="dabs_%d%d" % (g, jt))
             nc.scalar.activation(out=dabs[g, jt][:], in_=d_ps[:].rearrange("p (m t) -> p t m", t=PACK), func=ACT.Abs)
 
-        def invert(g, jt, bank):
-            x_ps = quad[bank]
+        def invert(g, jt, k):
+            x_ps = bank[k][:].rearrange("p (t j) -> p t j", t=PACK)
             for t in range(PACK):
                 nc.tensor.matmul(x_ps[:, t, :], b2[g, jt][:, t, :], ident[:], start=True, stop=False, is_transpose=True)
                 nc.tensor.matmul(x_ps[:, t, :], dabs[g, jt][:, t, :], ident[:], start=False, stop=True, is_transpose=True)
             root = ring.tile([P, P, PACK], F32, name="root")
             nc.scalar.activation(
-                out=root[:], in_=x_ps[:].rearrange("p t j -> p j t"), func=ACT.Abs_reciprocal_sqrt, bias=1.0,
+                out=root[:], in_=x_ps.rearrange("p t j -> p j t"), func=ACT.Abs_reciprocal_sqrt, bias=1.0,
             )
-            rec[g, jt] = keep.tile([P, P, PACK], F32, name="rec%d%d" % (g, jt))
+            rec[g, jt] = keep.tile([P, P, PACK], F32, name="rec%d%d" % (g, jt), tag="rec%d%d" % (g, jt), align_bytes=64)
             nc.scalar.activation(out=rec[g, jt][:], in_=root[:], func=ACT.Square)
 
         def prepare_w1(a, g):
-            w1_q[a, g] = quantize("w1_q%d%d" % (a, g), round_w1(nc.vector.tensor_copy, a, g))
+            w1_q[a, g] = quantize("w1_q%d%d" % (a, g), round_w1(a, g))
 
-        def quotient(g, jt, bank):
-            jh, u = divmod(jt, JH // P)
-            if u == 0:
-                h_bf[g, jh] = held("h_bf%d%d" % (g, jh), JH * PACK, BF16, "G%d" % jh if g == 0 else "")
+        def product_a(a, g, jt, k):
             j = slice(jt * P, (jt + 1) * P)
-            a_ps = quad[bank]
+            codes, plane = w1_q[a, g]
             for t in range(PACK):
                 cols = slice(t * P, (t + 1) * P)
-                for a in range(KPASS):
-                    codes, plane = w1_q[a, g]
-                    nc.tensor.matmul_mx(
-                        out=a_ps[:, t, :], lhsT=codes[:, cols].bitcast(FP8X4), lhsT_scale=plane[:, cols],
-                        rhs=v1[a][:, j].bitcast(FP8X4), rhs_scale=v1_s[4 * a :, j],
-                        start=(a == 0), stop=(a == KPASS - 1),
-                    )
+                nc.tensor.matmul_mx(
+                    out=bank[k][:, cols], lhsT=codes[:, cols].bitcast(FP8X4), lhsT_scale=plane[:, cols],
+                    rhs=v1[a][:, j].bitcast(FP8X4), rhs_scale=v1_s[4 * a :, j],
+                    start=(a == 0 and t == 0), stop=(a == KPASS - 1 and t == PACK - 1),
+                )
+
+        def quotient(g, jt, k):
+            jh, u = divmod(jt, JH // P)
+            if u == 0:
+                h_bf[g, jh] = held("h_bf%d%d" % (g, jh), JH * PACK, BF16)
             nc.vector.tensor_tensor(
                 out=h_bf[g, jh][:, u * KP : (u + 1) * KP].rearrange("p (j t) -> p j t", t=PACK),
-                in0=a_ps[:].rearrange("p t j -> p j t"), in1=rec[g, jt][:], op=ALU.mult,
+                in0=bank[k][:].rearrange("p (t j) -> p j t", t=PACK), in1=rec[g, jt][:], op=ALU.mult,
             )
 
         def quantize_h(g, jh):
@@ -197,7 +199,7 @@ def tile_list_cosolvent_well_quotient_kernel(
             for nt in range(N // P):
                 n = slice(nt * P, (nt + 1) * P)
                 nc.tensor.matmul_mx(
-                    out=o_ps[jh, nt // 2][:, nt % 2, :], lhsT=w4_w[:, g, n].bitcast(FP8X4), lhsT_scale=w4_s[4 * g :, n],
+                    out=bank[JT + 2 * jh + nt // 2][:, (nt % 2) * JH : (nt % 2 + 1) * JH], lhsT=w4_w[:, g, n].bitcast(FP8X4), lhsT_scale=w4_s[4 * g :, n],
                     rhs=codes[:].bitcast(FP8X4), rhs_scale=plane[:],
                     start=(g == 0 and nt % 2 == 0), stop=(g == HPASS - 1 and nt % 2 == 1),
                 )
@@ -205,12 +207,12 @@ def tile_list_cosolvent_well_quotient_kernel(
         def store(jh):
             for pair, copy in enumerate((nc.scalar.copy, nc.vector.tensor_copy if jh == 1 else nc.scalar.copy)):
                 res = keep.tile([P, 2, JH], F32, name="res%d%d" % (jh, pair))
-                copy(out=res[:], in_=o_ps[jh, pair][:])
+                copy(out=res[:], in_=bank[JT + 2 * jh + pair][:].rearrange("p (k j) -> p k j", k=2))
                 dst = out[pair * 2 * P : (pair + 1) * 2 * P, jh * JH : (jh + 1) * JH]
                 nc.sync.dma_start(out=dst.rearrange("(k p) j -> p k j", p=P), in_=res[:])
 
         b2, dabs, rec, w1_q, h_bf, h_q = {}, {}, {}, {}, {}, {}
-        quad = [psum.tile([P, PACK, P], F32, bufs=1, name="quad%d" % k) for k in range(4)]
+        bank = [psum.tile([P, KP], F32, bufs=1, name="bank%d" % k) for k in range(8)]
         v2 = gather("v2", tab2_w, list2, U32)
         v2_s = gather("v2_s", tab2_s, list2, U8)
         w3_q = [quantize("w3_q0", round_w3(nc.vector.tensor_copy, 0))]
@@ -218,40 +220,35 @@ def tile_list_cosolvent_well_quotient_kernel(
         v3_s = gather("v3_s", tab3_s, list3, U8, "X")
         for g in range(HPASS):
             for jt in range(JT):
-                square_b(g, jt)
+                square_b(g, jt, bank[jt])
         w3_q.append(quantize("w3_q1", round_w3(nc.vector.tensor_copy, 1)))
-        abs_d(0, 0)
-        abs_d(0, 1)
-        for jt in range(JT):
-            invert(0, jt, jt)
-            abs_d(*divmod(jt + 2, JT))
+        for g in range(HPASS):
+            for jt in range(JT):
+                abs_d(g, jt)
+        for g in range(HPASS):
+            for jt in range(JT):
+                invert(g, jt, JT * (1 - g) + jt)
         prepare_w1(0, 0)
         prepare_w1(1, 0)
         v1_s = gather("v1_s", tab_s, list1, U8, "Z")
         v1 = [gather("v1_%d" % a, tab_w[a], list1, U32, "YD"[a]) for a in range(KPASS)]
-        quotient(0, 0, 1)
-        quotient(0, 1, 2)
-        quantize_h(0, 0)
-        invert(1, 0, 0)
-        abs_d(1, 2)
-        quotient(0, 2, 3)
-        prepare_w1(0, 1)
-        invert(1, 1, 1)
-        abs_d(1, 3)
-        quotient(0, 3, 0)
-        quantize_h(0, 1)
-        invert(1, 2, 2)
-        invert(1, 3, 3)
+        for jt in range(JT):
+            for a in range(KPASS):
+                product_a(a, 0, jt, JT + jt)
+            quotient(0, jt, JT + jt)
+            if jt == 0:
+                prepare_w1(0, 1)
+            if jt % 2 == 1:
+                quantize_h(0, jt // 2)
+        for jt in range(JT):
+            product_a(0, 1, jt, jt)
         prepare_w1(1, 1)
-        o_ps = {}
-        for jh in range(2):
-            for pair in range(2):
-                o_ps[jh, pair] = psum.tile([P, 2, JH], F32, tag="wide", bufs=4, name="o_ps%d%d" % (jh, pair))
         for jh in range(2):
             features(0, jh)
         for jh in range(2):
-            quotient(1, 2 * jh, 2 * jh)
-            quotient(1, 2 * jh + 1, 2 * jh + 1)
+            for jt in (2 * jh, 2 * jh + 1):
+                product_a(1, 1, jt, jt)
+                quotient(1, jt, jt)
             quantize_h(1, jh)
             features(1, jh)
             store(jh)

@@ -143,7 +143,7 @@ def tile_list_cosolvent_well_quotient_kernel(
                 rhs=w2_w[:, r].bitcast(FP4X4), rhs_scale=w2_s[:, r], start=True, stop=True,
             )
             b2[g, jt] = keep.tile([P, PACK, P], F32, name="b2_%d%d" % (g, jt), tag="b2_%d%d" % (g, jt), align_bytes=64)
-            nc.scalar.activation(out=b2[g, jt][:], in_=b_ps[:].rearrange("p (m t) -> p t m", t=PACK), func=ACT.Square)
+            nc.scalar.activation(out=b2[g, jt][:].rearrange("p t m -> p m t"), in_=b_ps[:].rearrange("p (m t) -> p m t", t=PACK), func=ACT.Square)
 
         def abs_d(g, jt):
             d_ps = bank[jt]
@@ -154,7 +154,7 @@ def tile_list_cosolvent_well_quotient_kernel(
                 rhs=codes[:].bitcast(FP8X4), rhs_scale=plane[:], start=True, stop=True,
             )
             dabs[g, jt] = keep.tile([P, PACK, P], F32, name="dabs_%d%d" % (g, jt))
-            nc.scalar.activation(out=dabs[g, jt][:], in_=d_ps[:].rearrange("p (m t) -> p t m", t=PACK), func=ACT.Abs)
+            nc.scalar.activation(out=dabs[g, jt][:].rearrange("p t m -> p m t"), in_=d_ps[:].rearrange("p (m t) -> p m t", t=PACK), func=ACT.Abs)
 
         def invert(g, jt, k):
             x_ps = bank[k][:].rearrange("p (t j) -> p t j", t=PACK)

@@ -103,13 +103,12 @@ def tile_list_cosolvent_well_quotient_kernel(
         list3 = load_list("list3", offs3)
         w3_raw.append(load_weight("w3_raw1", w3, 0, 1))
         load_scales(nc.sync, tab3_s, tab3_scales)
-        w1_raw = {(a, 0): load_weight("w1_raw%d0" % a, w1, a, 0) for a in range(KPASS)}
+        w1_raw = {(0, 0): load_weight("w1_raw00", w1, 0, 0)}
         list1 = load_list("list1", offs)
         load_scales(nc.sync, tab_s, tab_scales)
-        tab_w = [
-            load_words("tab_w%d" % a, T, U32, tab_words[a].rearrange("p t i -> p (t i)"), "D" if a == 0 else "")
-            for a in range(KPASS)
-        ]
+        tab_w = [load_words("tab_w0", T, U32, tab_words[0].rearrange("p t i -> p (t i)"))]
+        w1_raw[1, 0] = load_weight("w1_raw10", w1, 1, 0)
+        tab_w.append(load_words("tab_w1", T, U32, tab_words[1].rearrange("p t i -> p (t i)")))
         for a in range(KPASS):
             w1_raw[a, 1] = load_weight("w1_raw%d1" % a, w1, a, 1)
         w4_w = keep.tile([P, HPASS, N], U32, name="w4_w", align_bytes=64)
@@ -125,12 +124,20 @@ def tile_list_cosolvent_well_quotient_kernel(
             return grouped
 
         def round_w1(a, g):
-            grouped = held("w1_bf%d%d" % (a, g), PACK * KP, BF16, "rec0%d" % (2 * a) if g == 1 else "ZY"[a])
+            grouped = held("w1_bf%d%d" % (a, g), PACK * KP, BF16, "Z" if (a, g) == (0, 0) else "w1_bf%d%d" % (a, g))
             dst = grouped[:].rearrange("p (t m i) -> p m i t", t=PACK, i=PACK)
             src = w1_raw[a, g][:].rearrange("p i (m t) -> p m i t", t=PACK)
             if (a, g) == (KPASS - 1, HPASS - 1):
                 nc.vector.tensor_copy(out=dst[:, :, :, 0:2], in_=src[:, :, :, 0:2])
-                nc.scalar.copy(out=dst[:, :, :, 2:4], in_=src[:, :, :, 2:4])
+                nc.gpsimd.tensor_scalar(
+                    out=dst[:, :, :, 2:4].rearrange("p m i t -> p t m i"), in0=src[:, :, :, 2:4].rearrange("p m i t -> p t m i"),
+                    scalar1=1.0, scalar2=0.0, op0=ALU.mult, op1=ALU.add,
+                )
+            elif g == 1:
+                nc.gpsimd.tensor_scalar(
+                    out=dst.rearrange("p m i t -> p t m i"), in0=src.rearrange("p m i t -> p t m i"),
+                    scalar1=1.0, scalar2=0.0, op0=ALU.mult, op1=ALU.add,
+                )
             else:
                 nc.vector.tensor_copy(out=dst, in_=src)
             return grouped
@@ -156,11 +163,19 @@ def tile_list_cosolvent_well_quotient_kernel(
             dabs[g, jt] = keep.tile([P, PACK, P], F32, name="dabs_%d%d" % (g, jt))
             nc.scalar.activation(out=dabs[g, jt][:].rearrange("p t m -> p m t"), in_=d_ps[:].rearrange("p (m t) -> p m t", t=PACK), func=ACT.Abs)
 
-        def invert(g, jt, k):
+        def turn(term, k, first):
             x_ps = bank[k][:].rearrange("p (t j) -> p t j", t=PACK)
             for t in range(PACK):
-                nc.tensor.matmul(x_ps[:, t, :], b2[g, jt][:, t, :], ident[:], start=True, stop=False, is_transpose=True)
-                nc.tensor.matmul(x_ps[:, t, :], dabs[g, jt][:, t, :], ident[:], start=False, stop=True, is_transpose=True)
+                nc.tensor.matmul(
+                    x_ps[:, t, :], term[:, t, :], ident[:], is_transpose=True,
+                    start=(first and t == 0), stop=(not first and t == PACK - 1),
+                )
+
+        def invert(g, jt, k):
+            x_ps = bank[k][:].rearrange("p (t j) -> p t j", t=PACK)
+            if g > 0:
+                turn(b2[g, jt], k, True)
+                turn(dabs[g, jt], k, False)
             root = ring.tile([P, P, PACK], F32, name="root")
             nc.scalar.activation(
                 out=root[:], in_=x_ps.rearrange("p t j -> p j t"), func=ACT.Abs_reciprocal_sqrt, bias=1.0,
@@ -183,16 +198,20 @@ def tile_list_cosolvent_well_quotient_kernel(
                 )
 
         def quotient(g, jt, k):
-            jh, u = divmod(jt, JH // P)
-            if u == 0:
-                h_bf[g, jh] = held("h_bf%d%d" % (g, jh), JH * PACK, BF16)
             nc.vector.tensor_tensor(
-                out=h_bf[g, jh][:, u * KP : (u + 1) * KP].rearrange("p (j t) -> p j t", t=PACK),
+                out=h_bf[g][:, jt * KP : (jt + 1) * KP].rearrange("p (j t) -> p j t", t=PACK),
                 in0=bank[k][:].rearrange("p (t j) -> p j t", t=PACK), in1=rec[g, jt][:], op=ALU.mult,
             )
 
-        def quantize_h(g, jh):
-            h_q[g, jh] = quantize("h_q%d%d" % (g, jh), h_bf[g, jh])
+        def quantize_h(g, lo, hi):
+            codes = held("h_codes%d%d" % (g, lo), (hi - lo) * JH, U32, "w1_bf11" if g == 0 else "")
+            plane = held("h_plane%d%d" % (g, lo), (hi - lo) * JH, U8)
+            nc.vector.quantize_mx(
+                out=codes[:].bitcast(FP8X4), scales=plane[:], in_=h_bf[g][:, lo * JH * PACK : hi * JH * PACK],
+            )
+            for jh in range(lo, hi):
+                j = slice((jh - lo) * JH, (jh - lo + 1) * JH)
+                h_q[g, jh] = codes[:, j], plane[:, j]
 
         def features(g, jh):
             codes, plane = h_q[g, jh]
@@ -200,7 +219,7 @@ def tile_list_cosolvent_well_quotient_kernel(
                 n = slice(nt * P, (nt + 1) * P)
                 nc.tensor.matmul_mx(
                     out=bank[JT + 2 * jh + nt // 2][:, (nt % 2) * JH : (nt % 2 + 1) * JH], lhsT=w4_w[:, g, n].bitcast(FP8X4), lhsT_scale=w4_s[4 * g :, n],
-                    rhs=codes[:].bitcast(FP8X4), rhs_scale=plane[:],
+                    rhs=codes.bitcast(FP8X4), rhs_scale=plane,
                     start=(g == 0 and nt % 2 == 0), stop=(g == HPASS - 1 and nt % 2 == 1),
                 )
 
@@ -211,7 +230,8 @@ def tile_list_cosolvent_well_quotient_kernel(
                 dst = out[pair * 2 * P : (pair + 1) * 2 * P, jh * JH : (jh + 1) * JH]
                 nc.sync.dma_start(out=dst.rearrange("(k p) j -> p k j", p=P), in_=res[:])
 
-        b2, dabs, rec, w1_q, h_bf, h_q = {}, {}, {}, {}, {}, {}
+        b2, dabs, rec, w1_q, h_q = {}, {}, {}, {}, {}
+        h_bf = [held("h_bf%d" % g, S * PACK, BF16) for g in range(HPASS)]
         bank = [psum.tile([P, KP], F32, bufs=1, name="bank%d" % k) for k in range(8)]
         v2 = gather("v2", tab2_w, list2, U32)
         v2_s = gather("v2_s", tab2_s, list2, U8)
@@ -221,34 +241,40 @@ def tile_list_cosolvent_well_quotient_kernel(
         for g in range(HPASS):
             for jt in range(JT):
                 square_b(g, jt, bank[jt])
+        for jt in range(JT):
+            turn(b2[0, jt], JT + jt, True)
         w3_q.append(quantize("w3_q1", round_w3(nc.vector.tensor_copy, 1)))
         for g in range(HPASS):
             for jt in range(JT):
                 abs_d(g, jt)
+        for jt in range(JT):
+            turn(dabs[0, jt], JT + jt, False)
         for g in range(HPASS):
             for jt in range(JT):
                 invert(g, jt, JT * (1 - g) + jt)
         prepare_w1(0, 0)
-        prepare_w1(1, 0)
         v1_s = gather("v1_s", tab_s, list1, U8, "Z")
-        v1 = [gather("v1_%d" % a, tab_w[a], list1, U32, "YD"[a]) for a in range(KPASS)]
+        v1 = [gather("v1_0", tab_w[0], list1, U32)]
         for jt in range(JT):
-            for a in range(KPASS):
-                product_a(a, 0, jt, JT + jt)
+            product_a(0, 0, jt, JT + jt)
+        prepare_w1(1, 0)
+        v1.append(gather("v1_1", tab_w[1], list1, U32))
+        for jt in range(JT):
+            product_a(1, 0, jt, JT + jt)
             quotient(0, jt, JT + jt)
             if jt == 0:
                 prepare_w1(0, 1)
-            if jt % 2 == 1:
-                quantize_h(0, jt // 2)
         for jt in range(JT):
             product_a(0, 1, jt, jt)
         prepare_w1(1, 1)
+        for jt in range(JT):
+            product_a(1, 1, jt, jt)
+        quantize_h(0, 0, 2)
         for jh in range(2):
             features(0, jh)
         for jh in range(2):
             for jt in (2 * jh, 2 * jh + 1):
-                product_a(1, 1, jt, jt)
                 quotient(1, jt, jt)
-            quantize_h(1, jh)
+            quantize_h(1, jh, jh + 1)
             features(1, jh)
             store(jh)

@@ -109,8 +109,13 @@ def tile_list_cosolvent_well_quotient_kernel(
         tab_w = [load_words("tab_w0", T, U32, tab_words[0].rearrange("p t i -> p (t i)"))]
         w1_raw[1, 0] = load_weight("w1_raw10", w1, 1, 0)
         tab_w.append(load_words("tab_w1", T, U32, tab_words[1].rearrange("p t i -> p (t i)")))
-        for a in range(KPASS):
-            w1_raw[a, 1] = load_weight("w1_raw%d1" % a, w1, a, 1)
+        w1_raw[0, 1] = load_weight("w1_raw01", w1, 0, 1)
+        last_raw = []
+        for half in range(2):
+            raw = keep.tile([P, PACK, KP // 2], F32, name="last_raw%d" % half, tag="last_raw%d" % half, align_bytes=64)
+            c0 = KP + half * KP // 2
+            nc.sync.dma_start(out=raw[:], in_=w1[KP:, c0 : c0 + KP // 2].rearrange("(p i) c -> p i c", i=PACK))
+            last_raw.append(raw)
         w4_w = keep.tile([P, HPASS, N], U32, name="w4_w", align_bytes=64)
         nc.sync.dma_start(out=w4_w[:].bitcast(I32), in_=w4_words.rearrange("g p n i -> p g (n i)").bitcast(I32))
         load_scales(nc.sync, w4_s, w4_scales)
@@ -124,22 +129,19 @@ def tile_list_cosolvent_well_quotient_kernel(
             return grouped
 
         def round_w1(a, g):
-            grouped = held("w1_bf%d%d" % (a, g), PACK * KP, BF16, "Z" if (a, g) == (0, 0) else "w1_bf%d%d" % (a, g))
+            grouped = held("w1_bf%d%d" % (a, g), PACK * KP, BF16, {(0, 0): "Z"}.get((a, g), "w1_bf%d%d" % (a, g)))
             dst = grouped[:].rearrange("p (t m i) -> p m i t", t=PACK, i=PACK)
-            src = w1_raw[a, g][:].rearrange("p i (m t) -> p m i t", t=PACK)
             if (a, g) == (KPASS - 1, HPASS - 1):
-                nc.vector.tensor_copy(out=dst[:, :, :, 0:2], in_=src[:, :, :, 0:2])
-                nc.gpsimd.tensor_scalar(
-                    out=dst[:, :, :, 2:4].rearrange("p m i t -> p t m i"), in0=src[:, :, :, 2:4].rearrange("p m i t -> p t m i"),
-                    scalar1=1.0, scalar2=0.0, op0=ALU.mult, op1=ALU.add,
-                )
-            elif g == 1:
-                nc.gpsimd.tensor_scalar(
-                    out=dst.rearrange("p m i t -> p t m i"), in0=src.rearrange("p m i t -> p t m i"),
-                    scalar1=1.0, scalar2=0.0, op0=ALU.mult, op1=ALU.add,
-                )
+                for half, copy in enumerate((nc.scalar.copy, nc.vector.tensor_copy)):
+                    src = last_raw[half][:].rearrange("p i (m t) -> p m i t", t=PACK)
+                    copy(out=dst[:, half * P // 2 : (half + 1) * P // 2], in_=src)
+            elif g == HPASS - 1:
+                src = w1_raw[a, g][:].rearrange("p i (m t) -> p m i t", t=PACK)
+                for half, copy in enumerate((nc.scalar.copy, nc.vector.tensor_copy)):
+                    m = slice(half * P // 2, (half + 1) * P // 2)
+                    copy(out=dst[:, m], in_=src[:, m])
             else:
-                nc.vector.tensor_copy(out=dst, in_=src)
+                nc.vector.tensor_copy(out=dst, in_=w1_raw[a, g][:].rearrange("p i (m t) -> p m i t", t=PACK))
             return grouped
 
         def square_b(g, jt, b_ps):
@@ -176,7 +178,10 @@ def tile_list_cosolvent_well_quotient_kernel(
             if g > 0:
                 turn(b2[g, jt], k, True)
                 turn(dabs[g, jt], k, False)
-            root = ring.tile([P, P, PACK], F32, name="root")
+            if (g, jt) == (1, 2):
+                root = keep.tile([P, P, PACK], F32, name="root12", tag="last_raw0", align_bytes=64)
+            else:
+                root = ring.tile([P, P, PACK], F32, name="root")
             nc.scalar.activation(
                 out=root[:], in_=x_ps.rearrange("p t j -> p j t"), func=ACT.Abs_reciprocal_sqrt, bias=1.0,
             )
@@ -204,31 +209,37 @@ def tile_list_cosolvent_well_quotient_kernel(
             )
 
         def quantize_h(g, lo, hi):
-            codes = held("h_codes%d%d" % (g, lo), (hi - lo) * JH, U32, "w1_bf11" if g == 0 else "")
-            plane = held("h_plane%d%d" % (g, lo), (hi - lo) * JH, U8)
+            codes = held("h_codes%d%d" % (g, lo), (hi - lo) * P, U32, "w1_bf11" if g == 0 else "")
+            plane = held("h_plane%d%d" % (g, lo), (hi - lo) * P, U8)
             nc.vector.quantize_mx(
-                out=codes[:].bitcast(FP8X4), scales=plane[:], in_=h_bf[g][:, lo * JH * PACK : hi * JH * PACK],
+                out=codes[:].bitcast(FP8X4), scales=plane[:], in_=h_bf[g][:, lo * KP : hi * KP],
             )
-            for jh in range(lo, hi):
-                j = slice((jh - lo) * JH, (jh - lo + 1) * JH)
-                h_q[g, jh] = codes[:, j], plane[:, j]
+            h_q[g] = codes, plane, lo
 
-        def features(g, jh):
-            codes, plane = h_q[g, jh]
+        def features(g, lo, hi, banks):
+            codes, plane, first = h_q[g]
+            j = slice((lo - first) * P, (hi - first) * P)
+            width = (hi - lo) * P
+            per = N // P // len(banks)
             for nt in range(N // P):
                 n = slice(nt * P, (nt + 1) * P)
                 nc.tensor.matmul_mx(
-                    out=bank[JT + 2 * jh + nt // 2][:, (nt % 2) * JH : (nt % 2 + 1) * JH], lhsT=w4_w[:, g, n].bitcast(FP8X4), lhsT_scale=w4_s[4 * g :, n],
-                    rhs=codes.bitcast(FP8X4), rhs_scale=plane,
-                    start=(g == 0 and nt % 2 == 0), stop=(g == HPASS - 1 and nt % 2 == 1),
+                    out=bank[banks[nt // per]][:, (nt % per) * width : (nt % per + 1) * width],
+                    lhsT=w4_w[:, g, n].bitcast(FP8X4), lhsT_scale=w4_s[4 * g :, n],
+                    rhs=codes[:, j].bitcast(FP8X4), rhs_scale=plane[:, j],
+                    start=(g == 0 and nt % per == 0), stop=(g == HPASS - 1 and nt % per == per - 1),
                 )
 
-        def store(jh):
-            for pair, copy in enumerate((nc.scalar.copy, nc.vector.tensor_copy if jh == 1 else nc.scalar.copy)):
-                res = keep.tile([P, 2, JH], F32, name="res%d%d" % (jh, pair))
-                copy(out=res[:], in_=bank[JT + 2 * jh + pair][:].rearrange("p (k j) -> p k j", k=2))
-                dst = out[pair * 2 * P : (pair + 1) * 2 * P, jh * JH : (jh + 1) * JH]
-                nc.sync.dma_start(out=dst.rearrange("(k p) j -> p k j", p=P), in_=res[:])
+        def store(lo, hi, banks):
+            width = (hi - lo) * P
+            res = keep.tile([P, N // P, width], F32, name="res%d" % lo)
+            per = N // P // len(banks)
+            for u, (k, copy) in enumerate(zip(banks, (nc.scalar.copy, nc.vector.tensor_copy))):
+                copy(
+                    out=res[:, per * u : per * (u + 1), :],
+                    in_=bank[k][:, : per * width].rearrange("p (k j) -> p k j", k=per),
+                )
+            nc.sync.dma_start(out=out[:, lo * P : hi * P].rearrange("(k p) j -> p k j", p=P), in_=res[:])
 
         b2, dabs, rec, w1_q, h_q = {}, {}, {}, {}, {}
         h_bf = [held("h_bf%d" % g, S * PACK, BF16) for g in range(HPASS)]
@@ -249,9 +260,10 @@ def tile_list_cosolvent_well_quotient_kernel(
                 abs_d(g, jt)
         for jt in range(JT):
             turn(dabs[0, jt], JT + jt, False)
-        for g in range(HPASS):
-            for jt in range(JT):
-                invert(g, jt, JT * (1 - g) + jt)
+        for jt in range(JT):
+            invert(0, jt, JT + jt)
+        for jt in range(2):
+            invert(1, jt, jt)
         prepare_w1(0, 0)
         v1_s = gather("v1_s", tab_s, list1, U8, "Z")
         v1 = [gather("v1_0", tab_w[0], list1, U32)]
@@ -259,22 +271,31 @@ def tile_list_cosolvent_well_quotient_kernel(
             product_a(0, 0, jt, JT + jt)
         prepare_w1(1, 0)
         v1.append(gather("v1_1", tab_w[1], list1, U32))
+        late_bf = round_w1(0, 1)
+        last_bf = round_w1(1, 1)
         for jt in range(JT):
             product_a(1, 0, jt, JT + jt)
             quotient(0, jt, JT + jt)
+            if jt < 2:
+                invert(1, 2 + jt, JT + jt)
             if jt == 0:
-                prepare_w1(0, 1)
+                w1_q[0, 1] = quantize("w1_q01", late_bf)
         for jt in range(JT):
             product_a(0, 1, jt, jt)
-        prepare_w1(1, 1)
+        w1_q[1, 1] = quantize("w1_q11", last_bf)
         for jt in range(JT):
             product_a(1, 1, jt, jt)
-        quantize_h(0, 0, 2)
-        for jh in range(2):
-            features(0, jh)
-        for jh in range(2):
-            for jt in (2 * jh, 2 * jh + 1):
-                quotient(1, jt, jt)
-            quantize_h(1, jh, jh + 1)
-            features(1, jh)
-            store(jh)
+        quantize_h(0, 0, JT)
+        parts = ((0, 1, (6,)), (1, 2, (7,)), (2, 3, (4, 5)), (3, 4, (0, 1)))
+        for part in parts[:3]:
+            features(0, *part)
+        for jt in range(2):
+            quotient(1, jt, jt)
+        features(0, *parts[3])
+        for lo, hi, banks in parts:
+            quantize_h(1, lo, hi)
+            if hi + 1 < JT:
+                quotient(1, hi + 1, hi + 1)
+            features(1, lo, hi, banks)
+        for part in parts:
+            store(*part)

@@ -45,9 +45,9 @@ def tile_list_cosolvent_well_quotient_kernel(
             engine.memset(plane[:].bitcast(I32), 0)
             return plane
 
-        def load_scales(queue, plane, scales):
+        def load_scales(queue, plane, scales, quadrants=range(4)):
             passes = scales.shape[0]
-            for q in range(4):
+            for q in quadrants:
                 queue.dma_start(
                     out=plane[32 * q : 32 * q + 4 * passes, :].bitcast(I32),
                     in_=scales[:, 4 * q : 4 * q + 4, :].bitcast(I32),
@@ -93,22 +93,23 @@ def tile_list_cosolvent_well_quotient_kernel(
 
         ident = keep.tile([P, P], F32, name="ident")
         make_identity(nc, ident[:])
+        w3_raw, w1_raw, tab_w = {}, {}, {}
         list2 = load_list("list2", offs2)
         tab2_w = load_words("tab2_w", T2, U32, tab2_words[0].rearrange("p t i -> p (t i)"))
         load_scales(nc.sync, tab2_s, tab2_scales)
         w2_w = load_words("w2_w", H, U16, w2_words[0])
-        w3_raw = [load_weight("w3_raw0", w3, 0, 0)]
+        w3_raw[0] = load_weight("w3_raw0", w3, 0, 0)
         load_scales(nc.sync, w2_s, w2_scales)
         tab3_w = load_words("tab3_w", T3, U16, tab3_words[0])
         list3 = load_list("list3", offs3)
-        w3_raw.append(load_weight("w3_raw1", w3, 0, 1))
+        w3_raw[1] = load_weight("w3_raw1", w3, 0, 1)
         load_scales(nc.sync, tab3_s, tab3_scales)
-        w1_raw = {(0, 0): load_weight("w1_raw00", w1, 0, 0)}
+        w1_raw[0, 0] = load_weight("w1_raw00", w1, 0, 0)
+        tab_w[0] = load_words("tab_w0", T, U32, tab_words[0].rearrange("p t i -> p (t i)"))
         list1 = load_list("list1", offs)
         load_scales(nc.sync, tab_s, tab_scales)
-        tab_w = [load_words("tab_w0", T, U32, tab_words[0].rearrange("p t i -> p (t i)"))]
         w1_raw[1, 0] = load_weight("w1_raw10", w1, 1, 0)
-        tab_w.append(load_words("tab_w1", T, U32, tab_words[1].rearrange("p t i -> p (t i)")))
+        tab_w[1] = load_words("tab_w1", T, U32, tab_words[1].rearrange("p t i -> p (t i)"))
         w1_raw[0, 1] = load_weight("w1_raw01", w1, 0, 1)
         last_raw = []
         for half in range(2):
@@ -255,12 +256,15 @@ def tile_list_cosolvent_well_quotient_kernel(
         for jt in range(JT):
             turn(b2[0, jt], JT + jt, True)
         w3_q.append(quantize("w3_q1", round_w3(nc.vector.tensor_copy, 1)))
-        for g in range(HPASS):
-            for jt in range(JT):
-                abs_d(g, jt)
+        for jt in range(JT):
+            abs_d(0, jt)
         for jt in range(JT):
             turn(dabs[0, jt], JT + jt, False)
+        for jt in range(2):
+            invert(0, jt, JT + jt)
         for jt in range(JT):
+            abs_d(1, jt)
+        for jt in range(2, JT):
             invert(0, jt, JT + jt)
         for jt in range(2):
             invert(1, jt, jt)

@@ -179,8 +179,8 @@ def tile_list_cosolvent_well_quotient_kernel(
             if g > 0:
                 turn(b2[g, jt], k, True)
                 turn(dabs[g, jt], k, False)
-            if (g, jt) == (1, 2):
-                root = keep.tile([P, P, PACK], F32, name="root12", tag="last_raw0", align_bytes=64)
+            if (g, jt) == (1, 1):
+                root = keep.tile([P, P, PACK], F32, name="root11", tag="last_raw0", align_bytes=64)
             else:
                 root = ring.tile([P, P, PACK], F32, name="root")
             nc.scalar.activation(
@@ -266,8 +266,7 @@ def tile_list_cosolvent_well_quotient_kernel(
             abs_d(1, jt)
         for jt in range(2, JT):
             invert(0, jt, JT + jt)
-        for jt in range(2):
-            invert(1, jt, jt)
+        invert(1, 0, 0)
         prepare_w1(0, 0)
         v1_s = gather("v1_s", tab_s, list1, U8, "Z")
         v1 = [gather("v1_0", tab_w[0], list1, U32)]
@@ -280,8 +279,8 @@ def tile_list_cosolvent_well_quotient_kernel(
         for jt in range(JT):
             product_a(1, 0, jt, JT + jt)
             quotient(0, jt, JT + jt)
-            if jt < 2:
-                invert(1, 2 + jt, JT + jt)
+            if jt < JT - 1:
+                invert(1, 1 + jt, JT + jt)
             if jt == 0:
                 w1_q[0, 1] = quantize("w1_q01", late_bf)
         for jt in range(JT):
@@ -290,7 +289,7 @@ def tile_list_cosolvent_well_quotient_kernel(
         for jt in range(JT):
             product_a(1, 1, jt, jt)
         quantize_h(0, 0, JT)
-        parts = ((0, 1, (6,)), (1, 2, (7,)), (2, 3, (4, 5)), (3, 4, (0, 1)))
+        parts = ((0, 1, (7,)), (1, 2, (4,)), (2, 3, (5, 6)), (3, 4, (0, 1)))
         for part in parts[:3]:
             features(0, *part)
         for jt in range(2):

@@ -53,6 +53,10 @@ def tile_list_cosolvent_well_quotient_kernel(
                     in_=scales[:, 4 * q : 4 * q + 4, :].bitcast(I32),
                 )
 
+        def load_plane(plane, scales):
+            for r in range(4):
+                nc.sync.dma_start(out=plane[r:P:32, :].bitcast(I32), in_=scales[0, r:16:4, :].bitcast(I32))
+
         def load_words(name, cols, dtype, src, slot=""):
             words = held(name, cols, dtype, slot)
             nc.sync.dma_start(out=words[:].bitcast(I32), in_=src.bitcast(I32))
@@ -96,14 +100,14 @@ def tile_list_cosolvent_well_quotient_kernel(
         w3_raw, w1_raw, tab_w = {}, {}, {}
         list2 = load_list("list2", offs2)
         tab2_w = load_words("tab2_w", T2, U32, tab2_words[0].rearrange("p t i -> p (t i)"))
-        load_scales(nc.sync, tab2_s, tab2_scales)
+        load_plane(tab2_s, tab2_scales)
         w2_w = load_words("w2_w", H, U16, w2_words[0])
         w3_raw[0] = load_weight("w3_raw0", w3, 0, 0)
-        load_scales(nc.sync, w2_s, w2_scales)
+        load_plane(w2_s, w2_scales)
         tab3_w = load_words("tab3_w", T3, U16, tab3_words[0])
         list3 = load_list("list3", offs3)
         w3_raw[1] = load_weight("w3_raw1", w3, 0, 1)
-        load_scales(nc.sync, tab3_s, tab3_scales)
+        load_plane(tab3_s, tab3_scales)
         w1_raw[0, 0] = load_weight("w1_raw00", w1, 0, 0)
         tab_w[0] = load_words("tab_w0", T, U32, tab_words[0].rearrange("p t i -> p (t i)"))
         list1 = load_list("list1", offs)

@@ -78,6 +78,12 @@ def tile_list_cosolvent_well_quotient_kernel(
             nc.vector.tensor_copy(picked[:], window[:].indirect(offsets[:]))
             return picked
 
+        def gather_half(picked, window, offsets, half):
+            nc.vector.tensor_copy(
+                picked[:, half * JH : (half + 1) * JH],
+                window[:].indirect(offsets[:, half * JH // 16 : (half + 1) * JH // 16]),
+            )
+
         def quantize(name, grouped):
             cols = grouped.shape[1] // PACK
             codes = held(name + "_codes", cols, U32)
@@ -277,7 +283,9 @@ def tile_list_cosolvent_well_quotient_kernel(
         for jt in range(JT):
             product_a(0, 0, jt, JT + jt)
         prepare_w1(1, 0)
-        v1.append(gather("v1_1", tab_w[1], list1, U32))
+        v1.append(held("v1_1", S, U32))
+        for half in range(2):
+            gather_half(v1[1], tab_w[1], list1, half)
         late_bf = round_w1(0, 1)
         last_bf = round_w1(1, 1)
         for jt in range(JT):
@@ -294,15 +302,13 @@ def tile_list_cosolvent_well_quotient_kernel(
             product_a(1, 1, jt, jt)
         quantize_h(0, 0, JT)
         parts = ((0, 1, (7,)), (1, 2, (4,)), (2, 3, (5, 6)), (3, 4, (0, 1)))
-        for part in parts[:3]:
-            features(0, *part)
         for jt in range(2):
             quotient(1, jt, jt)
-        features(0, *parts[3])
         for lo, hi, banks in parts:
             quantize_h(1, lo, hi)
             if hi + 1 < JT:
                 quotient(1, hi + 1, hi + 1)
-            features(1, lo, hi, banks)
+            for g in range(HPASS):
+                features(g, lo, hi, banks)
         for part in parts:
             store(*part)

@@ -24,6 +24,7 @@ KPASS = K // KP
 HPASS = H // KP
 JT = S // P
 JH = S // 2
+SHARE = 80
 
 
 def tile_list_cosolvent_well_quotient_kernel(
@@ -148,8 +149,7 @@ def tile_list_cosolvent_well_quotient_kernel(
                     copy(out=dst[:, half * P // 2 : (half + 1) * P // 2], in_=src)
             elif g == HPASS - 1:
                 src = w1_raw[a, g][:].rearrange("p i (m t) -> p m i t", t=PACK)
-                for half, copy in enumerate((nc.scalar.copy, nc.vector.tensor_copy)):
-                    m = slice(half * P // 2, (half + 1) * P // 2)
+                for copy, m in ((nc.scalar.copy, slice(0, SHARE)), (nc.vector.tensor_copy, slice(SHARE, P))):
                     copy(out=dst[:, m], in_=src[:, m])
             else:
                 nc.vector.tensor_copy(out=dst, in_=w1_raw[a, g][:].rearrange("p i (m t) -> p m i t", t=PACK))
@@ -262,7 +262,7 @@ def tile_list_cosolvent_well_quotient_kernel(
         v3_s = gather("v3_s", tab3_s, list3, U8, "X")
         for g in range(HPASS):
             for jt in range(JT):
-                square_b(g, jt, bank[jt])
+                square_b(g, jt, bank[(1 - g) * JT + jt])
         for jt in range(JT):
             turn(b2[0, jt], JT + jt, True)
         w3_q.append(quantize("w3_q1", round_w3(nc.vector.tensor_copy, 1)))

@@ -270,13 +270,10 @@ def tile_list_cosolvent_well_quotient_kernel(
             abs_d(0, jt)
         for jt in range(JT):
             turn(dabs[0, jt], JT + jt, False)
-        for jt in range(2):
+        for jt in range(JT):
             invert(0, jt, JT + jt)
         for jt in range(JT):
             abs_d(1, jt)
-        for jt in range(2, JT):
-            invert(0, jt, JT + jt)
-        invert(1, 0, 0)
         prepare_w1(0, 0)
         v1_s = gather("v1_s", tab_s, list1, U8, "Z")
         v1 = [gather("v1_0", tab_w[0], list1, U32)]
@@ -291,8 +288,7 @@ def tile_list_cosolvent_well_quotient_kernel(
         for jt in range(JT):
             product_a(1, 0, jt, JT + jt)
             quotient(0, jt, JT + jt)
-            if jt < JT - 1:
-                invert(1, 1 + jt, JT + jt)
+            invert(1, jt, JT + jt)
             if jt == 0:
                 w1_q[0, 1] = quantize("w1_q01", late_bf)
         for jt in range(JT):
@@ -301,7 +297,7 @@ def tile_list_cosolvent_well_quotient_kernel(
         for jt in range(JT):
             product_a(1, 1, jt, jt)
         quantize_h(0, 0, JT)
-        parts = ((0, 1, (7,)), (1, 2, (4,)), (2, 3, (5, 6)), (3, 4, (0, 1)))
+        parts = ((0, 1, (4,)), (1, 2, (5,)), (2, 3, (6, 7)), (3, 4, (0, 1)))
         for jt in range(2):
             quotient(1, jt, jt)
         for lo, hi, banks in parts:

@@ -23,7 +23,6 @@ KP = P * PACK
 KPASS = K // KP
 HPASS = H // KP
 JT = S // P
-JH = S // 2
 SHARE = 80
 
 
@@ -79,11 +78,8 @@ def tile_list_cosolvent_well_quotient_kernel(
             nc.vector.tensor_copy(picked[:], window[:].indirect(offsets[:]))
             return picked
 
-        def gather_half(picked, window, offsets, half):
-            nc.vector.tensor_copy(
-                picked[:, half * JH : (half + 1) * JH],
-                window[:].indirect(offsets[:, half * JH // 16 : (half + 1) * JH // 16]),
-            )
+        def gather_part(picked, window, offsets, lo, hi):
+            nc.vector.tensor_copy(picked[:, lo * P : hi * P], window[:].indirect(offsets[:, lo * P // 16 : hi * P // 16]))
 
         def quantize(name, grouped):
             cols = grouped.shape[1] // PACK
@@ -135,8 +131,8 @@ def tile_list_cosolvent_well_quotient_kernel(
         def round_w3(copy, g):
             grouped = held("w3_bf%d" % g, PACK * KP, BF16, "XZ"[g])
             copy(
-                out=grouped[:].rearrange("p (c e i) -> p c i e", e=4, i=PACK),
-                in_=w3_raw[g][:].rearrange("p i (c e) -> p c i e", e=4),
+                out=grouped[:].rearrange("p (t m i) -> p m i t", t=PACK, i=PACK),
+                in_=w3_raw[g][:].rearrange("p i (m t) -> p m i t", t=PACK),
             )
             return grouped
 
@@ -174,7 +170,7 @@ def tile_list_cosolvent_well_quotient_kernel(
                 rhs=codes[:].bitcast(FP8X4), rhs_scale=plane[:], start=True, stop=True,
             )
             dabs[g, jt] = keep.tile([P, PACK, P], F32, name="dabs_%d%d" % (g, jt))
-            nc.scalar.activation(out=dabs[g, jt][:].rearrange("p t m -> p m t"), in_=d_ps[:].rearrange("p (m t) -> p m t", t=PACK), func=ACT.Abs)
+            nc.scalar.activation(out=dabs[g, jt][:].rearrange("p t m -> p (t m)"), in_=d_ps[:], func=ACT.Abs)
 
         def turn(term, k, first):
             x_ps = bank[k][:].rearrange("p (t j) -> p t j", t=PACK)
@@ -281,8 +277,8 @@ def tile_list_cosolvent_well_quotient_kernel(
             product_a(0, 0, jt, JT + jt)
         prepare_w1(1, 0)
         v1.append(held("v1_1", S, U32))
-        for half in range(2):
-            gather_half(v1[1], tab_w[1], list1, half)
+        for lo, hi in ((0, 1), (1, 2), (2, 4)):
+            gather_part(v1[1], tab_w[1], list1, lo, hi)
         late_bf = round_w1(0, 1)
         last_bf = round_w1(1, 1)
         for jt in range(JT):

@@ -23,7 +23,9 @@ KP = P * PACK
 KPASS = K // KP
 HPASS = H // KP
 JT = S // P
-SHARE = 80
+SHARE = 72
+LAST_SHARES = (48, 18)
+UNIT_BYTES = KP * 4
 
 
 def tile_list_cosolvent_well_quotient_kernel(
@@ -34,6 +36,7 @@ def tile_list_cosolvent_well_quotient_kernel(
     with ExitStack() as ctx:
         lists = ctx.enter_context(tc.tile_pool(name="lists", bufs=1))
         keep = ctx.enter_context(tc.tile_pool(name="keep", bufs=1))
+        late = ctx.enter_context(tc.tile_pool(name="late", bufs=1))
         ring = ctx.enter_context(tc.tile_pool(name="ring", bufs=3))
         psum = ctx.enter_context(tc.psum_pool(name="psum", bufs=2))
 
@@ -120,7 +123,7 @@ def tile_list_cosolvent_well_quotient_kernel(
         w1_raw[0, 1] = load_weight("w1_raw01", w1, 0, 1)
         last_raw = []
         for half in range(2):
-            raw = keep.tile([P, PACK, KP // 2], F32, name="last_raw%d" % half, tag="last_raw%d" % half, align_bytes=64)
+            raw = late.tile([P, PACK, KP // 2], F32, name="last_raw%d" % half, offset=2 * half * UNIT_BYTES)
             c0 = KP + half * KP // 2
             nc.sync.dma_start(out=raw[:], in_=w1[KP:, c0 : c0 + KP // 2].rearrange("(p i) c -> p i c", i=PACK))
             last_raw.append(raw)
@@ -140,9 +143,11 @@ def tile_list_cosolvent_well_quotient_kernel(
             grouped = held("w1_bf%d%d" % (a, g), PACK * KP, BF16, {(0, 0): "Z"}.get((a, g), "w1_bf%d%d" % (a, g)))
             dst = grouped[:].rearrange("p (t m i) -> p m i t", t=PACK, i=PACK)
             if (a, g) == (KPASS - 1, HPASS - 1):
-                for half, copy in enumerate((nc.scalar.copy, nc.vector.tensor_copy)):
+                for half, share in enumerate(LAST_SHARES):
                     src = last_raw[half][:].rearrange("p i (m t) -> p m i t", t=PACK)
-                    copy(out=dst[:, half * P // 2 : (half + 1) * P // 2], in_=src)
+                    piece = dst[:, half * P // 2 : (half + 1) * P // 2]
+                    nc.scalar.copy(out=piece[:, :share], in_=src[:, :share])
+                    nc.vector.tensor_copy(out=piece[:, share:], in_=src[:, share:])
             elif g == HPASS - 1:
                 src = w1_raw[a, g][:].rearrange("p i (m t) -> p m i t", t=PACK)
                 for copy, m in ((nc.scalar.copy, slice(0, SHARE)), (nc.vector.tensor_copy, slice(SHARE, P))):
@@ -185,8 +190,8 @@ def tile_list_cosolvent_well_quotient_kernel(
             if g > 0:
                 turn(b2[g, jt], k, True)
                 turn(dabs[g, jt], k, False)
-            if (g, jt) == (1, 1):
-                root = keep.tile([P, P, PACK], F32, name="root11", tag="last_raw0", align_bytes=64)
+            if g == 1 and jt > 0:
+                root = late.tile([P, P, PACK], F32, name="late_root%d" % jt, offset=(2 + jt % 2) * UNIT_BYTES)
             else:
                 root = ring.tile([P, P, PACK], F32, name="root")
             nc.scalar.activation(
@@ -266,15 +271,17 @@ def tile_list_cosolvent_well_quotient_kernel(
             abs_d(0, jt)
         for jt in range(JT):
             turn(dabs[0, jt], JT + jt, False)
+        abs_d(1, 0)
         for jt in range(JT):
             invert(0, jt, JT + jt)
-        for jt in range(JT):
+        for jt in range(1, JT):
             abs_d(1, jt)
         prepare_w1(0, 0)
         v1_s = gather("v1_s", tab_s, list1, U8, "Z")
         v1 = [gather("v1_0", tab_w[0], list1, U32)]
         for jt in range(JT):
             product_a(0, 0, jt, JT + jt)
+        invert(1, 0, 0)
         prepare_w1(1, 0)
         v1.append(held("v1_1", S, U32))
         for lo, hi in ((0, 1), (1, 2), (2, 4)):
@@ -284,8 +291,9 @@ def tile_list_cosolvent_well_quotient_kernel(
         for jt in range(JT):
             product_a(1, 0, jt, JT + jt)
             quotient(0, jt, JT + jt)
-            invert(1, jt, JT + jt)
-            if jt == 0:
+            if jt > 0:
+                invert(1, jt, JT + jt)
+            else:
                 w1_q[0, 1] = quantize("w1_q01", late_bf)
         for jt in range(JT):
             product_a(0, 1, jt, jt)

@@ -23,8 +23,8 @@ KP = P * PACK
 KPASS = K // KP
 HPASS = H // KP
 JT = S // P
-SHARE = 72
-LAST_SHARES = (48, 18)
+SHARE = 80
+GPSIMD_SQUARES = 2
 UNIT_BYTES = KP * 4
 
 
@@ -143,11 +143,9 @@ def tile_list_cosolvent_well_quotient_kernel(
             grouped = held("w1_bf%d%d" % (a, g), PACK * KP, BF16, {(0, 0): "Z"}.get((a, g), "w1_bf%d%d" % (a, g)))
             dst = grouped[:].rearrange("p (t m i) -> p m i t", t=PACK, i=PACK)
             if (a, g) == (KPASS - 1, HPASS - 1):
-                for half, share in enumerate(LAST_SHARES):
+                for half, copy in enumerate((nc.scalar.copy, nc.vector.tensor_copy)):
                     src = last_raw[half][:].rearrange("p i (m t) -> p m i t", t=PACK)
-                    piece = dst[:, half * P // 2 : (half + 1) * P // 2]
-                    nc.scalar.copy(out=piece[:, :share], in_=src[:, :share])
-                    nc.vector.tensor_copy(out=piece[:, share:], in_=src[:, share:])
+                    copy(out=dst[:, half * P // 2 : (half + 1) * P // 2], in_=src)
             elif g == HPASS - 1:
                 src = w1_raw[a, g][:].rearrange("p i (m t) -> p m i t", t=PACK)
                 for copy, m in ((nc.scalar.copy, slice(0, SHARE)), (nc.vector.tensor_copy, slice(SHARE, P))):
@@ -191,14 +189,18 @@ def tile_list_cosolvent_well_quotient_kernel(
                 turn(b2[g, jt], k, True)
                 turn(dabs[g, jt], k, False)
             if g == 1 and jt > 0:
-                root = late.tile([P, P, PACK], F32, name="late_root%d" % jt, offset=(2 + jt % 2) * UNIT_BYTES)
+                root = late.tile([P, P, PACK], F32, name="late_root%d" % jt, offset=(jt % 2) * UNIT_BYTES)
+            elif g == 0 and jt < GPSIMD_SQUARES:
+                root = keep.tile([P, P, PACK], F32, name="first_root%d" % jt)
+                first_roots.append(root)
             else:
                 root = ring.tile([P, P, PACK], F32, name="root")
             nc.scalar.activation(
                 out=root[:], in_=x_ps.rearrange("p t j -> p j t"), func=ACT.Abs_reciprocal_sqrt, bias=1.0,
             )
-            rec[g, jt] = keep.tile([P, P, PACK], F32, name="rec%d%d" % (g, jt), tag="rec%d%d" % (g, jt), align_bytes=64)
-            nc.scalar.activation(out=rec[g, jt][:], in_=root[:], func=ACT.Square)
+            if g > 0 or jt >= GPSIMD_SQUARES:
+                rec[g, jt] = keep.tile([P, P, PACK], F32, name="rec%d%d" % (g, jt))
+                nc.scalar.activation(out=rec[g, jt][:], in_=root[:], func=ACT.Square)
 
         def prepare_w1(a, g):
             w1_q[a, g] = quantize("w1_q%d%d" % (a, g), round_w1(a, g))
@@ -253,7 +255,7 @@ def tile_list_cosolvent_well_quotient_kernel(
                 )
             nc.sync.dma_start(out=out[:, lo * P : hi * P].rearrange("(k p) j -> p k j", p=P), in_=res[:])
 
-        b2, dabs, rec, w1_q, h_q = {}, {}, {}, {}, {}
+        b2, dabs, rec, w1_q, h_q, first_roots = {}, {}, {}, {}, {}, []
         h_bf = [held("h_bf%d" % g, S * PACK, BF16) for g in range(HPASS)]
         bank = [psum.tile([P, KP], F32, bufs=1, name="bank%d" % k) for k in range(8)]
         v2 = gather("v2", tab2_w, list2, U32)
@@ -277,7 +279,10 @@ def tile_list_cosolvent_well_quotient_kernel(
         for jt in range(1, JT):
             abs_d(1, jt)
         prepare_w1(0, 0)
-        v1_s = gather("v1_s", tab_s, list1, U8, "Z")
+        for jt, root in enumerate(first_roots):
+            rec[0, jt] = keep.tile([P, P, PACK], F32, name="rec0%d" % jt, tag=("Z", "rec01")[jt], align_bytes=64)
+            nc.gpsimd.tensor_tensor(out=rec[0, jt][:], in0=root[:], in1=root[:], op=ALU.mult)
+        v1_s = gather("v1_s", tab_s, list1, U8)
         v1 = [gather("v1_0", tab_w[0], list1, U32)]
         for jt in range(JT):
             product_a(0, 0, jt, JT + jt)

@@ -23,8 +23,9 @@ KP = P * PACK
 KPASS = K // KP
 HPASS = H // KP
 JT = S // P
-SHARE = 80
+SHARE = 68
 GPSIMD_SQUARES = 2
+LAST_SHARE = 18
 UNIT_BYTES = KP * 4
 
 
@@ -143,9 +144,10 @@ def tile_list_cosolvent_well_quotient_kernel(
             grouped = held("w1_bf%d%d" % (a, g), PACK * KP, BF16, {(0, 0): "Z"}.get((a, g), "w1_bf%d%d" % (a, g)))
             dst = grouped[:].rearrange("p (t m i) -> p m i t", t=PACK, i=PACK)
             if (a, g) == (KPASS - 1, HPASS - 1):
-                for half, copy in enumerate((nc.scalar.copy, nc.vector.tensor_copy)):
-                    src = last_raw[half][:].rearrange("p i (m t) -> p m i t", t=PACK)
-                    copy(out=dst[:, half * P // 2 : (half + 1) * P // 2], in_=src)
+                src = [raw[:].rearrange("p i (m t) -> p m i t", t=PACK) for raw in last_raw]
+                nc.scalar.copy(out=dst[:, : P // 2], in_=src[0])
+                nc.scalar.copy(out=dst[:, P // 2 : P // 2 + LAST_SHARE], in_=src[1][:, :LAST_SHARE])
+                nc.vector.tensor_copy(out=dst[:, P // 2 + LAST_SHARE :], in_=src[1][:, LAST_SHARE:])
             elif g == HPASS - 1:
                 src = w1_raw[a, g][:].rearrange("p i (m t) -> p m i t", t=PACK)
                 for copy, m in ((nc.scalar.copy, slice(0, SHARE)), (nc.vector.tensor_copy, slice(SHARE, P))):
@@ -189,7 +191,7 @@ def tile_list_cosolvent_well_quotient_kernel(
                 turn(b2[g, jt], k, True)
                 turn(dabs[g, jt], k, False)
             if g == 1 and jt > 0:
-                root = late.tile([P, P, PACK], F32, name="late_root%d" % jt, offset=(jt % 2) * UNIT_BYTES)
+                root = late.tile([P, P, PACK], F32, name="late_root%d" % jt, offset=(2 + jt % 2) * UNIT_BYTES)
             elif g == 0 and jt < GPSIMD_SQUARES:
                 root = keep.tile([P, P, PACK], F32, name="first_root%d" % jt)
                 first_roots.append(root)
@@ -202,13 +204,22 @@ def tile_list_cosolvent_well_quotient_kernel(
                 rec[g, jt] = keep.tile([P, P, PACK], F32, name="rec%d%d" % (g, jt))
                 nc.scalar.activation(out=rec[g, jt][:], in_=root[:], func=ACT.Square)
 
+        def quantize_by_slices(name, grouped):
+            codes, plane = held(name + "_codes", KP, U32), held(name + "_plane", KP, U8)
+            for t in range(PACK):
+                cols = slice(t * P, (t + 1) * P)
+                nc.vector.quantize_mx(
+                    out=codes[:, cols].bitcast(FP8X4), scales=plane[:, cols], in_=grouped[:, t * KP : (t + 1) * KP],
+                )
+            return codes, plane
+
         def prepare_w1(a, g):
             w1_q[a, g] = quantize("w1_q%d%d" % (a, g), round_w1(a, g))
 
-        def product_a(a, g, jt, k):
+        def product_a(a, g, jt, k, slices=range(PACK)):
             j = slice(jt * P, (jt + 1) * P)
             codes, plane = w1_q[a, g]
-            for t in range(PACK):
+            for t in slices:
                 cols = slice(t * P, (t + 1) * P)
                 nc.tensor.matmul_mx(
                     out=bank[k][:, cols], lhsT=codes[:, cols].bitcast(FP8X4), lhsT_scale=plane[:, cols],
@@ -299,9 +310,10 @@ def tile_list_cosolvent_well_quotient_kernel(
             if jt > 0:
                 invert(1, jt, JT + jt)
             else:
-                w1_q[0, 1] = quantize("w1_q01", late_bf)
-        for jt in range(JT):
-            product_a(0, 1, jt, jt)
+                w1_q[0, 1] = quantize_by_slices("w1_q01", late_bf)
+        for t in range(PACK):
+            for jt in range(JT):
+                product_a(0, 1, jt, jt, (t,))
         w1_q[1, 1] = quantize("w1_q11", last_bf)
         for jt in range(JT):
             product_a(1, 1, jt, jt)

from contextlib import ExitStack

import concourse.mybir as mybir
from concourse.masks import make_identity

K, M, H, N, T, T2, T3, S = 1024, 512, 1024, 512, 2048, 1024, 1024, 512
FLOPS = 2 * S * H * (K + 2 * M + N)

F32 = mybir.dt.float32
BF16 = mybir.dt.bfloat16
I32 = mybir.dt.int32
U32 = mybir.dt.uint32
U16 = mybir.dt.uint16
U8 = mybir.dt.uint8
FP8X4 = mybir.dt.float8_e4m3fn_x4
FP4X4 = mybir.dt.float4_e2m1fn_x4
ACT = mybir.ActivationFunctionType
ALU = mybir.AluOpType

P = 128
PACK = 4
KP = P * PACK
KPASS = K // KP
HPASS = H // KP
JT = S // P
SHARE = 68
GPSIMD_SQUARES = 2
LAST_SHARE = 18
UNIT_BYTES = KP * 4


def tile_list_cosolvent_well_quotient_kernel(
    tc, tab_words, tab_scales, tab2_words, tab2_scales, tab3_words, tab3_scales,
    offs, offs2, offs3, w1, w2_words, w2_scales, w3, w4_words, w4_scales, out,
):
    nc = tc.nc
    with ExitStack() as ctx:
        lists = ctx.enter_context(tc.tile_pool(name="lists", bufs=1))
        keep = ctx.enter_context(tc.tile_pool(name="keep", bufs=1))
        late = ctx.enter_context(tc.tile_pool(name="late", bufs=1))
        ring = ctx.enter_context(tc.tile_pool(name="ring", bufs=3))
        psum = ctx.enter_context(tc.psum_pool(name="psum", bufs=2))

        def held(name, cols, dtype, slot=""):
            return keep.tile([P, cols], dtype, name=name, tag=slot, align_bytes=64)

        def zeroed_plane(engine, name, cols, slot=""):
            plane = held(name, cols, U8, slot)
            engine.memset(plane[:].bitcast(I32), 0)
            return plane

        def load_scales(queue, plane, scales, quadrants=range(4)):
            passes = scales.shape[0]
            for q in quadrants:
                queue.dma_start(
                    out=plane[32 * q : 32 * q + 4 * passes, :].bitcast(I32),
                    in_=scales[:, 4 * q : 4 * q + 4, :].bitcast(I32),
                )

        def load_plane(plane, scales):
            for r in range(4):
                nc.sync.dma_start(out=plane[r:P:32, :].bitcast(I32), in_=scales[0, r:16:4, :].bitcast(I32))

        def load_words(name, cols, dtype, src, slot=""):
            words = held(name, cols, dtype, slot)
            nc.sync.dma_start(out=words[:].bitcast(I32), in_=src.bitcast(I32))
            return words

        def load_list(name, src):
            tile = lists.tile([P, S // 16], U16, name=name)
            nc.sync.dma_start(tile[:], src)
            return tile

        def load_weight(name, w, a, g):
            raw = keep.tile([P, PACK, KP], F32, name=name)
            src = w[a * KP : (a + 1) * KP, g * KP : (g + 1) * KP]
            nc.sync.dma_start(out=raw[:], in_=src.rearrange("(p i) c -> p i c", i=PACK))
            return raw

        def gather(name, window, offsets, dtype, slot=""):
            picked = held(name, S, dtype, slot)
            nc.vector.tensor_copy(picked[:], window[:].indirect(offsets[:]))
            return picked

        def gather_part(picked, window, offsets, lo, hi):
            nc.vector.tensor_copy(picked[:, lo * P : hi * P], window[:].indirect(offsets[:, lo * P // 16 : hi * P // 16]))

        def quantize(name, grouped):
            cols = grouped.shape[1] // PACK
            codes = held(name + "_codes", cols, U32)
            plane = held(name + "_plane", cols, U8)
            nc.vector.quantize_mx(out=codes[:].bitcast(FP8X4), scales=plane[:], in_=grouped[:])
            return codes, plane

        tab2_s = zeroed_plane(nc.vector, "tab2_s", T2)
        w2_s = zeroed_plane(nc.gpsimd, "w2_s", H)
        tab3_s = zeroed_plane(nc.vector, "tab3_s", T3, "Z")
        tab_s = zeroed_plane(nc.gpsimd, "tab_s", T)
        w4_s = zeroed_plane(nc.vector, "w4_s", N)

        warm = keep.tile([P, 2], F32, name="warm")
        nc.vector.memset(warm[:, 0:1], 1.0)
        nc.scalar.activation(out=warm[:, 1:2], in_=warm[:, 0:1], func=ACT.Abs_reciprocal_sqrt)

        ident = keep.tile([P, P], F32, name="ident")
        make_identity(nc, ident[:])
        w3_raw, w1_raw, tab_w = {}, {}, {}
        list2 = load_list("list2", offs2)
        tab2_w = load_words("tab2_w", T2, U32, tab2_words[0].rearrange("p t i -> p (t i)"))
        load_plane(tab2_s, tab2_scales)
        w2_w = load_words("w2_w", H, U16, w2_words[0])
        w3_raw[0] = load_weight("w3_raw0", w3, 0, 0)
        load_plane(w2_s, w2_scales)
        tab3_w = load_words("tab3_w", T3, U16, tab3_words[0])
        list3 = load_list("list3", offs3)
        w3_raw[1] = load_weight("w3_raw1", w3, 0, 1)
        load_plane(tab3_s, tab3_scales)
        w1_raw[0, 0] = load_weight("w1_raw00", w1, 0, 0)
        tab_w[0] = load_words("tab_w0", T, U32, tab_words[0].rearrange("p t i -> p (t i)"))
        list1 = load_list("list1", offs)
        load_scales(nc.sync, tab_s, tab_scales)
        w1_raw[1, 0] = load_weight("w1_raw10", w1, 1, 0)
        tab_w[1] = load_words("tab_w1", T, U32, tab_words[1].rearrange("p t i -> p (t i)"))
        w1_raw[0, 1] = load_weight("w1_raw01", w1, 0, 1)
        last_raw = []
        for half in range(2):
            raw = late.tile([P, PACK, KP // 2], F32, name="last_raw%d" % half, offset=2 * half * UNIT_BYTES)
            c0 = KP + half * KP // 2
            nc.sync.dma_start(out=raw[:], in_=w1[KP:, c0 : c0 + KP // 2].rearrange("(p i) c -> p i c", i=PACK))
            last_raw.append(raw)
        w4_w = keep.tile([P, HPASS, N], U32, name="w4_w", align_bytes=64)
        nc.sync.dma_start(out=w4_w[:].bitcast(I32), in_=w4_words.rearrange("g p n i -> p g (n i)").bitcast(I32))
        load_scales(nc.sync, w4_s, w4_scales)

        def round_w3(copy, g):
            grouped = held("w3_bf%d" % g, PACK * KP, BF16, "XZ"[g])
            copy(
                out=grouped[:].rearrange("p (t m i) -> p m i t", t=PACK, i=PACK),
                in_=w3_raw[g][:].rearrange("p i (m t) -> p m i t", t=PACK),
            )
            return grouped

        def round_w1(a, g):
            grouped = held("w1_bf%d%d" % (a, g), PACK * KP, BF16, {(0, 0): "Z"}.get((a, g), "w1_bf%d%d" % (a, g)))
            dst = grouped[:].rearrange("p (t m i) -> p m i t", t=PACK, i=PACK)
            if (a, g) == (KPASS - 1, HPASS - 1):
                src = [raw[:].rearrange("p i (m t) -> p m i t", t=PACK) for raw in last_raw]
                nc.scalar.copy(out=dst[:, : P // 2], in_=src[0])
                nc.scalar.copy(out=dst[:, P // 2 : P // 2 + LAST_SHARE], in_=src[1][:, :LAST_SHARE])
                nc.vector.tensor_copy(out=dst[:, P // 2 + LAST_SHARE :], in_=src[1][:, LAST_SHARE:])
            elif g == HPASS - 1:
                src = w1_raw[a, g][:].rearrange("p i (m t) -> p m i t", t=PACK)
                for copy, m in ((nc.scalar.copy, slice(0, SHARE)), (nc.vector.tensor_copy, slice(SHARE, P))):
                    copy(out=dst[:, m], in_=src[:, m])
            else:
                nc.vector.tensor_copy(out=dst, in_=w1_raw[a, g][:].rearrange("p i (m t) -> p m i t", t=PACK))
            return grouped

        def square_b(g, jt, b_ps):
            j = slice(jt * P, (jt + 1) * P)
            r = slice(g * KP, (g + 1) * KP)
            nc.tensor.matmul_mx(
                out=b_ps[:], lhsT=v2[:, j].bitcast(FP8X4), lhsT_scale=v2_s[:, j],
                rhs=w2_w[:, r].bitcast(FP4X4), rhs_scale=w2_s[:, r], start=True, stop=True,
            )
            b2[g, jt] = keep.tile([P, PACK, P], F32, name="b2_%d%d" % (g, jt), tag="b2_%d%d" % (g, jt), align_bytes=64)
            nc.scalar.activation(out=b2[g, jt][:].rearrange("p t m -> p m t"), in_=b_ps[:].rearrange("p (m t) -> p m t", t=PACK), func=ACT.Square)

        def abs_d(g, jt):
            d_ps = bank[jt]
            j = slice(jt * P, (jt + 1) * P)
            codes, plane = w3_q[g]
            nc.tensor.matmul_mx(
                out=d_ps[:], lhsT=v3[:, j].bitcast(FP4X4), lhsT_scale=v3_s[:, j],
                rhs=codes[:].bitcast(FP8X4), rhs_scale=plane[:], start=True, stop=True,
            )
            dabs[g, jt] = keep.tile([P, PACK, P], F32, name="dabs_%d%d" % (g, jt))
            nc.scalar.activation(out=dabs[g, jt][:].rearrange("p t m -> p (t m)"), in_=d_ps[:], func=ACT.Abs)

        def turn(term, k, first):
            x_ps = bank[k][:].rearrange("p (t j) -> p t j", t=PACK)
            for t in range(PACK):
                nc.tensor.matmul(
                    x_ps[:, t, :], term[:, t, :], ident[:], is_transpose=True,
                    start=(first and t == 0), stop=(not first and t == PACK - 1),
                )

        def invert(g, jt, k):
            x_ps = bank[k][:].rearrange("p (t j) -> p t j", t=PACK)
            if g > 0:
                turn(b2[g, jt], k, True)
                turn(dabs[g, jt], k, False)
            if g == 1 and jt > 0:
                root = late.tile([P, P, PACK], F32, name="late_root%d" % jt, offset=(2 + jt % 2) * UNIT_BYTES)
            elif g == 0 and jt < GPSIMD_SQUARES:
                root = keep.tile([P, P, PACK], F32, name="first_root%d" % jt)
                first_roots.append(root)
            else:
                root = ring.tile([P, P, PACK], F32, name="root")
            nc.scalar.activation(
                out=root[:], in_=x_ps.rearrange("p t j -> p j t"), func=ACT.Abs_reciprocal_sqrt, bias=1.0,
            )
            if g > 0 or jt >= GPSIMD_SQUARES:
                rec[g, jt] = keep.tile([P, P, PACK], F32, name="rec%d%d" % (g, jt))
                nc.scalar.activation(out=rec[g, jt][:], in_=root[:], func=ACT.Square)

        def quantize_by_slices(name, grouped):
            codes, plane = held(name + "_codes", KP, U32), held(name + "_plane", KP, U8)
            for t in range(PACK):
                cols = slice(t * P, (t + 1) * P)
                nc.vector.quantize_mx(
                    out=codes[:, cols].bitcast(FP8X4), scales=plane[:, cols], in_=grouped[:, t * KP : (t + 1) * KP],
                )
            return codes, plane

        def prepare_w1(a, g):
            w1_q[a, g] = quantize("w1_q%d%d" % (a, g), round_w1(a, g))

        def product_a(a, g, jt, k, slices=range(PACK)):
            j = slice(jt * P, (jt + 1) * P)
            codes, plane = w1_q[a, g]
            for t in slices:
                cols = slice(t * P, (t + 1) * P)
                nc.tensor.matmul_mx(
                    out=bank[k][:, cols], lhsT=codes[:, cols].bitcast(FP8X4), lhsT_scale=plane[:, cols],
                    rhs=v1[a][:, j].bitcast(FP8X4), rhs_scale=v1_s[4 * a :, j],
                    start=(a == 0 and t == 0), stop=(a == KPASS - 1 and t == PACK - 1),
                )

        def quotient(g, jt, k):
            nc.vector.tensor_tensor(
                out=h_bf[g][:, jt * KP : (jt + 1) * KP].rearrange("p (j t) -> p j t", t=PACK),
                in0=bank[k][:].rearrange("p (t j) -> p j t", t=PACK), in1=rec[g, jt][:], op=ALU.mult,
            )

        def quantize_h(g, lo, hi):
            codes = held("h_codes%d%d" % (g, lo), (hi - lo) * P, U32, "w1_bf11" if g == 0 else "")
            plane = held("h_plane%d%d" % (g, lo), (hi - lo) * P, U8)
            nc.vector.quantize_mx(
                out=codes[:].bitcast(FP8X4), scales=plane[:], in_=h_bf[g][:, lo * KP : hi * KP],
            )
            h_q[g] = codes, plane, lo

        def features(g, lo, hi, banks):
            codes, plane, first = h_q[g]
            j = slice((lo - first) * P, (hi - first) * P)
            width = (hi - lo) * P
            per = N // P // len(banks)
            for nt in range(N // P):
                n = slice(nt * P, (nt + 1) * P)
                nc.tensor.matmul_mx(
                    out=bank[banks[nt // per]][:, (nt % per) * width : (nt % per + 1) * width],
                    lhsT=w4_w[:, g, n].bitcast(FP8X4), lhsT_scale=w4_s[4 * g :, n],
                    rhs=codes[:, j].bitcast(FP8X4), rhs_scale=plane[:, j],
                    start=(g == 0 and nt % per == 0), stop=(g == HPASS - 1 and nt % per == per - 1),
                )

        def store(lo, hi, banks):
            width = (hi - lo) * P
            res = keep.tile([P, N // P, width], F32, name="res%d" % lo)
            per = N // P // len(banks)
            for u, (k, copy) in enumerate(zip(banks, (nc.scalar.copy, nc.vector.tensor_copy))):
                copy(
                    out=res[:, per * u : per * (u + 1), :],
                    in_=bank[k][:, : per * width].rearrange("p (k j) -> p k j", k=per),
                )
            nc.sync.dma_start(out=out[:, lo * P : hi * P].rearrange("(k p) j -> p k j", p=P), in_=res[:])

        b2, dabs, rec, w1_q, h_q, first_roots = {}, {}, {}, {}, {}, []
        h_bf = [held("h_bf%d" % g, S * PACK, BF16) for g in range(HPASS)]
        bank = [psum.tile([P, KP], F32, bufs=1, name="bank%d" % k) for k in range(8)]
        v2 = gather("v2", tab2_w, list2, U32)
        v2_s = gather("v2_s", tab2_s, list2, U8)
        w3_q = [quantize("w3_q0", round_w3(nc.vector.tensor_copy, 0))]
        v3 = gather("v3", tab3_w, list3, U16)
        v3_s = gather("v3_s", tab3_s, list3, U8, "X")
        for g in range(HPASS):
            for jt in range(JT):
                square_b(g, jt, bank[(1 - g) * JT + jt])
        for jt in range(JT):
            turn(b2[0, jt], JT + jt, True)
        w3_q.append(quantize("w3_q1", round_w3(nc.vector.tensor_copy, 1)))
        for jt in range(JT):
            abs_d(0, jt)
        for jt in range(JT):
            turn(dabs[0, jt], JT + jt, False)
        abs_d(1, 0)
        for jt in range(JT):
            invert(0, jt, JT + jt)
        for jt in range(1, JT):
            abs_d(1, jt)
        prepare_w1(0, 0)
        for jt, root in enumerate(first_roots):
            rec[0, jt] = keep.tile([P, P, PACK], F32, name="rec0%d" % jt, tag=("Z", "rec01")[jt], align_bytes=64)
            nc.gpsimd.tensor_tensor(out=rec[0, jt][:], in0=root[:], in1=root[:], op=ALU.mult)
        v1_s = gather("v1_s", tab_s, list1, U8)
        v1 = [gather("v1_0", tab_w[0], list1, U32)]
        for jt in range(JT):
            product_a(0, 0, jt, JT + jt)
        invert(1, 0, 0)
        prepare_w1(1, 0)
        v1.append(held("v1_1", S, U32))
        for lo, hi in ((0, 1), (1, 2), (2, 4)):
            gather_part(v1[1], tab_w[1], list1, lo, hi)
        late_bf = round_w1(0, 1)
        last_bf = round_w1(1, 1)
        for jt in range(JT):
            product_a(1, 0, jt, JT + jt)
            quotient(0, jt, JT + jt)
            if jt > 0:
                invert(1, jt, JT + jt)
            else:
                w1_q[0, 1] = quantize_by_slices("w1_q01", late_bf)
        for t in range(PACK):
            for jt in range(JT):
                product_a(0, 1, jt, jt, (t,))
        w1_q[1, 1] = quantize("w1_q11", last_bf)
        for jt in range(JT):
            product_a(1, 1, jt, jt)
        quantize_h(0, 0, JT)
        parts = ((0, 1, (4,)), (1, 2, (5,)), (2, 3, (6, 7)), (3, 4, (0, 1)))
        for jt in range(2):
            quotient(1, jt, jt)
        for lo, hi, banks in parts:
            quantize_h(1, lo, hi)
            if hi + 1 < JT:
                quotient(1, hi + 1, hi + 1)
            for g in range(HPASS):
                features(g, lo, hi, banks)
        for part in parts:
            store(*part)
